import numpy as np
import ml_dtypes


def mxq(x, axis, fmt="e4m3"):
    dtype, down = {"e4m3": (ml_dtypes.float8_e4m3fn, 7), "e5m2": (ml_dtypes.float8_e5m2, 14)}[fmt]
    v = np.moveaxis(np.asarray(x, np.float32).astype(ml_dtypes.bfloat16).astype(np.float64), axis, -1)
    blocks = v.reshape(v.shape[:-1] + (-1, 32))
    amax = np.abs(blocks).max(-1, keepdims=True)
    byte = np.maximum(np.where(amax > 0, np.frexp(amax)[1] - 1 + 127, 0) - down, 1)
    scale = np.exp2(byte - 127.0)
    codes = (blocks / scale).astype(np.float32).astype(dtype).astype(np.float64)
    return np.moveaxis((codes * scale).reshape(v.shape), -1, axis)


WIDE = False


def mx_kscale(k):
    if not WIDE:
        return np.ones(k)
    levels = np.array([10, -10, 5, -5, 0])
    if k % 512:
        return np.exp2(np.random.permutation(np.resize(levels, k // 32))).repeat(32)
    a = np.empty((k // 512, 16))
    for p in range(k // 512):
        a[p, :8] = np.random.permutation(np.resize(levels, 8))
        for g in range(8):
            far = levels[np.abs(levels - a[p, g]) >= 10]
            a[p, g + 8] = far[np.random.randint(len(far))]
    return np.exp2(a.ravel()).repeat(32)


def f64(x):
    return np.asarray(x).astype(np.float64)


def striped(idx):
    return np.tile(idx.reshape(-1, 16).T, (8, 1)).astype(np.uint16)


def unstriped(offs):
    return offs[:16].T.reshape(-1).astype(np.int64)


def striped8(idx):
    return np.concatenate([x.reshape(-1, 16).T for x in idx]).astype(np.uint16)


def runs(offs, k):
    lists = np.stack([offs[16 * r : 16 * r + 16].T.reshape(-1) for r in range(8)]).astype(np.int64)
    return lists[np.arange(k) % 512 // 64]


def pack_weight(w):
    k, n = w.shape
    w = f64(np.asarray(w, np.float32).astype(ml_dtypes.bfloat16)).reshape(k // 32, 32, n)
    amax = np.abs(w).max(1)
    byte = np.clip(np.where(amax > 0, np.frexp(amax)[1] - 1 + 127 - 7, 1), 1, 254)
    scaled = (w * np.exp2(127.0 - byte)[:, None, :]).reshape(k, n).astype(np.float32)
    words = np.ascontiguousarray(scaled.reshape(k // 512, 128, 4, n).transpose(0, 1, 3, 2)).astype(ml_dtypes.float8_e4m3fn).view(np.uint8)
    return words, np.ascontiguousarray(byte.astype(np.uint8).reshape(k // 512, 16, n))


def unpack_weight(words, scales):
    g, p, n, _ = words.shape
    vals = np.ascontiguousarray(words).view(ml_dtypes.float8_e4m3fn).astype(np.float64) * np.repeat(np.exp2(scales.astype(np.float64) - 127.0), 8, axis=1)[..., None]
    return vals.transpose(0, 1, 3, 2).reshape(g * 512, n)


def sigmoid(v):
    return 1.0 / (1.0 + np.exp(-np.maximum(v, -700.0)))


K, T, S, N, H = 512, 2048, 256, 512, 512


def setup_inputs():
    n = np.random.standard_normal
    s = mx_kscale(K)[:, None]
    u = mx_kscale(H)
    packed_xT = pack_weight(n((K, T)) * s)
    return {
        "x_words": packed_xT[0],
        "x_scales": packed_xT[1],
        "w1": (n((K, H)) / np.sqrt(K) / s).astype(np.float32),
        "w2": (n((K, H)) / np.sqrt(K) / s).astype(np.float32),
        "tau": np.random.uniform(0.3, 0.9, (H, 1)).astype(np.float32),
        "sl": np.random.uniform(1.0, 2.0, (H, 1)).astype(np.float32),
        "th": (0.5 * n((H, 1))).astype(np.float32),
        "gn": (np.random.uniform(0.5, 1.5, (H, 1)) * u[:, None]).astype(np.float32),
        "gm": (np.random.uniform(0.5, 1.5, (H, 1)) * u[:, None]).astype(np.float32),
        "w3": (n((H, N)) / np.sqrt(2 * H) / u[:, None]).astype(np.float32),
        "w4": (n((H, N)) / np.sqrt(2 * H) / u[:, None]).astype(np.float32),
        "offs": striped(np.random.permutation(T)[:S]),
        "hz": striped8(np.random.randint(0, T, (8, S))),
        "n1": striped8(np.stack([np.random.permutation(S) for _ in range(8)])),
        "n2": striped(np.random.permutation(S)),
        "n3": striped(np.random.permutation(S)),
        "n4": striped8(np.stack([np.random.permutation(S) for _ in range(8)])),
        "n5": striped8(np.stack([np.random.permutation(S) for _ in range(8)])),
    }


def reference(x_words, x_scales, w1, w2, tau, sl, th, gn, gm, w3, w4, offs, hz, n1, n2, n3, n4, n5):
    xq = unpack_weight(x_words, x_scales)[:, unstriped(offs)]
    y = mxq(f64(w1), 0, "e4m3").T @ xq
    top = y.max(axis=1, keepdims=True)
    ea = np.exp(f64(tau) * (y[np.arange(H)[:, None], runs(n1, H)] - top))
    z = f64(gn) * (2.0 * (y * ea))
    x_hz = unpack_weight(x_words, x_scales)[np.arange(K)[:, None], runs(hz, K)]
    d = mxq(f64(w2), 0, "e4m3").T @ x_hz
    sg = sigmoid(f64(sl) * (d[:, unstriped(n2)] - f64(th)))
    st = d * sg
    z2 = f64(gm) * (st - (0.5 * st[:, unstriped(n3)]))
    h = mxq(f64(w3), 0, "e4m3").T @ mxq(z, 0, "e4m3") + mxq(f64(w4), 0, "e4m3").T @ mxq(z2, 0, "e4m3")
    st2 = h[np.arange(N)[:, None], runs(n4, N)] - h
    return h * (sigmoid(st2[np.arange(N)[:, None], runs(n5, N)]))

@@ -1,0 +1,233 @@
+from contextlib import ExitStack
+
+import concourse.mybir as mybir
+
+K, T, S, N, H = 512, 2048, 256, 512, 512
+FLOPS = 4 * 2 * 512 * 512 * 256
+
+F32 = mybir.dt.float32
+BF16 = mybir.dt.bfloat16
+I32 = mybir.dt.int32
+U32 = mybir.dt.uint32
+U16 = mybir.dt.uint16
+U8 = mybir.dt.uint8
+FP8X4 = mybir.dt.float8_e4m3fn_x4
+ALU = mybir.AluOpType
+ACT = mybir.ActivationFunctionType
+
+P = 128
+PACK = 4
+
+
+def tile_picked_hjoinepkehphopd_none_p_kernel(
+    tc, x_words, x_scales, w1, w2, tau, sl, th, gn, gm, w3, w4, offs, hz, n1, n2, n3, n4, n5, out
+):
+    nc = tc.nc
+    with ExitStack() as ctx:
+        lists = ctx.enter_context(tc.tile_pool(name="lists", bufs=1))
+        sb = ctx.enter_context(tc.tile_pool(name="sb", bufs=1))
+        psum = ctx.enter_context(tc.psum_pool(name="psum", bufs=1))
+
+        def load_list(name, src):
+            tile = lists.tile([P, S // 16], U16, name=name)
+            nc.sync.dma_start(tile[:], src)
+            return tile
+
+        def load_part(name, w, u):
+            width = w.shape[1] // 2
+            raw = sb.tile([P, PACK, width], F32, name="%s_raw%d" % (name, u))
+            nc.sync.dma_start(raw[:], w[:, u * width : (u + 1) * width].rearrange("(p j) c -> p j c", j=PACK))
+            return raw
+
+        def load_gain(queue, name, v):
+            tile = sb.tile([P, PACK], F32, name=name)
+            queue.dma_start(tile[:], v.rearrange("(p t) o -> p (t o)", t=PACK))
+            return tile
+
+        def deal(engine, grouped, raw, u):
+            ms = raw.shape[2] // PACK
+            dst = grouped[:].rearrange("p (t m j) -> p m j t", t=PACK, j=PACK)[:, u * ms : (u + 1) * ms]
+            src = raw[:].rearrange("p j (m t) -> p m j t", t=PACK)
+            if engine == "gpsimd":
+                dst = dst.rearrange("p m j t -> p m t j")
+                src = src.rearrange("p m j t -> p m t j")
+                nc.gpsimd.tensor_scalar(dst, src, 1.0, 0.0, ALU.mult, ALU.add)
+            elif engine == "scalar":
+                nc.scalar.copy(dst, src)
+            else:
+                nc.vector.tensor_copy(dst, src)
+
+        def mx_tiles(name, cols):
+            grouped = sb.tile([P, PACK * cols], BF16, name=name + "_bf16", align_bytes=64)
+            codes = sb.tile([P, cols], U32, name=name + "_codes", align_bytes=64)
+            scales = sb.tile([P, cols], U8, name=name + "_scales", align_bytes=64)
+            return grouped, codes, scales
+
+        def quantize(tiles, c0, c1):
+            grouped, codes, scales = tiles
+            nc.vector.quantize_mx(codes[:, c0:c1].bitcast(FP8X4), scales[:, c0:c1], grouped[:, PACK * c0 : PACK * c1])
+
+        def product(acc, w_tiles, t, codes, scales, start, stop):
+            cols = slice(t * P, (t + 1) * P)
+            nc.tensor.matmul_mx(
+                out=acc[:],
+                lhsT=w_tiles[1][:, cols].bitcast(FP8X4),
+                lhsT_scale=w_tiles[2][:, cols],
+                rhs=codes[:].bitcast(FP8X4),
+                rhs_scale=scales[:],
+                start=start,
+                stop=stop,
+            )
+
+        def interleave(engine, grouped, planes):
+            dst = grouped[:].rearrange("p (c i t) -> p c t i", t=PACK, i=4)
+            src = planes[:].rearrange("p t (c i) -> p c t i", i=4)
+            if engine == "scalar":
+                nc.scalar.copy(dst, src)
+            else:
+                nc.vector.tensor_copy(dst, src)
+
+        planes = range(PACK)
+
+        xs = sb.tile([P, T], U8, name="xs")
+        nc.vector.memset(xs[:].bitcast(I32), 0)
+        w1_raw = [load_part("w1", w1, 0)]
+        offs_t = load_list("offs_t", offs)
+        hz_t = load_list("hz_t", hz)
+        n1_t = load_list("n1_t", n1)
+        n2_t = load_list("n2_t", n2)
+        n3_t = load_list("n3_t", n3)
+        n4_t = load_list("n4_t", n4)
+        w1_raw.append(load_part("w1", w1, 1))
+        xw = sb.tile([P, T], I32, name="xw")
+        nc.sync.dma_start(xw[:], x_words[0].rearrange("p c r -> p (c r)").bitcast(I32))
+        for r in range(4):
+            nc.scalar.dma_start(xs[r:P:32, :].bitcast(I32), x_scales[0][r:16:4, :].bitcast(I32))
+        for r in (2, 3):
+            nc.scalar.dma_start(xs[14 + r : P : 32, :].bitcast(I32), x_scales[0][r:16:4, :].bitcast(I32))
+        tau_t = load_gain(nc.gpsimd, "tau_t", tau)
+        gn_t = load_gain(nc.gpsimd, "gn_t", gn)
+        w2_raw = [load_part("w2", w2, u) for u in range(2)]
+        sl_t = load_gain(nc.sync, "sl_t", sl)
+        th_t = load_gain(nc.sync, "th_t", th)
+        gm_t = load_gain(nc.sync, "gm_t", gm)
+        w3_raw = [load_part("w3", w3, u) for u in range(2)]
+        w4_raw = [load_part("w4", w4, u) for u in range(2)]
+        n5_t = load_list("n5_t", n5)
+
+        y_win = [sb.tile([P, 2 * S], F32, name="y_win%d" % t) for t in planes]
+        d_win = [sb.tile([P, 2 * S], F32, name="d_win%d" % t) for t in planes]
+        st_win = [sb.tile([P, 2 * S], F32, name="st_win%d" % t) for t in planes]
+        for t in planes:
+            nc.vector.memset(y_win[t][:, S:], 0.0)
+
+        w1_mx = mx_tiles("w1", H)
+        for u in range(2):
+            deal("vector", w1_mx[0], w1_raw[u], u)
+        xq_scales = sb.tile([P, S], U8, name="xq_scales", align_bytes=64)
+        nc.vector.tensor_copy(xq_scales[:], xs[:].indirect(offs_t[:]))
+        quantize(w1_mx, 0, H)
+        xh_picked = sb.tile([P, S], U8, name="xh_picked", align_bytes=64)
+        nc.vector.tensor_copy(xh_picked[:], xs[:].indirect(hz_t[:]))
+        xh_scales = sb.tile([P, S], U8, name="xh_scales", align_bytes=64)
+        nc.vector.tensor_copy(xh_scales[:].bitcast(I32), xh_picked[:].bitcast(I32))
+        for r in (2, 3):
+            nc.gpsimd.dma_start(xh_scales[r:P:32, :].bitcast(I32), xh_picked[14 + r : P : 32, :].bitcast(I32))
+        ntau = sb.tile([P, PACK], F32, name="ntau")
+        nc.vector.tensor_scalar(ntau[:], tau_t[:], -1.0, None, ALU.mult)
+        gn2 = sb.tile([P, PACK], F32, name="gn2")
+        nc.vector.tensor_scalar(gn2[:], gn_t[:], 2.0, None, ALU.mult)
+
+        xq_words = sb.tile([P, S], U32, name="xq_words", align_bytes=64)
+        nc.vector.tensor_copy(xq_words[:], xw[:].bitcast(U32).indirect(offs_t[:]))
+        y_ps = [psum.tile([P, S], F32, name="y_ps%d" % t, tag="bank%d" % t) for t in planes]
+        for t in planes:
+            product(y_ps[t], w1_mx, t, xq_words, xq_scales, True, True)
+        xh_words = sb.tile([P, S], U32, name="xh_words", align_bytes=64)
+        nc.vector.tensor_copy(xh_words[:], xw[:].bitcast(U32).indirect(hz_t[:]))
+        w2_mx = mx_tiles("w2", H)
+        for u in range(2):
+            deal("gpsimd", w2_mx[0], w2_raw[u], u)
+        top = [sb.tile([P, 1], F32, name="top%d" % t) for t in planes]
+        ea_bias = [sb.tile([P, 1], F32, name="ea_bias%d" % t) for t in planes]
+        for t in planes:
+            nc.vector.tensor_scalar(y_win[t][:, :S], y_ps[t][:], 1.0, None, ALU.mult, ALU.max, accum_out=top[t][:])
+            nc.vector.tensor_scalar(ea_bias[t][:], top[t][:], ntau[:, t : t + 1], None, ALU.mult)
+            nc.scalar.activation(
+                d_win[t][:, S:], y_win[t][:].indirect(n1_t[:]), ACT.Exp, bias=ea_bias[t][:], scale=tau_t[:, t : t + 1]
+            )
+        z_planes = sb.tile([P, PACK, S], F32, name="z_planes")
+        for t in planes:
+            nc.vector.scalar_tensor_tensor(
+                z_planes[:, t, :], y_ps[t][:], gn2[:, t : t + 1], d_win[t][:, S:], ALU.mult, ALU.mult
+            )
+
+        sg_bias = sb.tile([P, PACK], F32, name="sg_bias")
+        nc.vector.scalar_tensor_tensor(sg_bias[:], sl_t[:], -1.0, th_t[:], ALU.mult, ALU.mult)
+        d_ps = [psum.tile([P, S], F32, name="d_ps%d" % t, tag="bank%d" % (PACK + t)) for t in planes]
+        for t in planes:
+            quantize(w2_mx, t * P, (t + 1) * P)
+            product(d_ps[t], w2_mx, t, xh_words, xh_scales, True, True)
+        w3_mx = mx_tiles("w3", N)
+        for u in range(2):
+            deal("gpsimd", w3_mx[0], w3_raw[u], u)
+        for t in planes:
+            nc.vector.tensor_copy(d_win[t][:, :S], d_ps[t][:])
+            nc.scalar.activation(
+                st_win[t][:, S:],
+                d_win[t][:].indirect(n2_t[:]),
+                ACT.Sigmoid,
+                bias=sg_bias[:, t : t + 1],
+                scale=sl_t[:, t : t + 1],
+            )
+        z_mx = mx_tiles("z", S)
+        interleave("vector", z_mx[0], z_planes)
+        far = sb.tile([P, PACK, S], F32, name="far")
+        z2_planes = sb.tile([P, PACK, S], F32, name="z2_planes")
+        for t in planes:
+            nc.vector.scalar_tensor_tensor(
+                st_win[t][:, :S], d_ps[t][:], gm_t[:, t : t + 1], st_win[t][:, S:], ALU.mult, ALU.mult
+            )
+            nc.scalar.activation(far[:, t, :], st_win[t][:].indirect(n3_t[:]), ACT.Copy)
+        quantize(z_mx, 0, S)
+        quantize(w3_mx, 0, N)
+        h_ps = [psum.tile([P, S], F32, name="h_ps%d" % t, tag="bank%d" % t) for t in planes]
+        for t in planes:
+            product(h_ps[t], w3_mx, t, z_mx[1], z_mx[2], True, False)
+        w4_mx = mx_tiles("w4", N)
+        for u in range(2):
+            deal("vector", w4_mx[0], w4_raw[u], u)
+        for t in planes:
+            nc.vector.scalar_tensor_tensor(
+                z2_planes[:, t, :], far[:, t, :], -0.5, st_win[t][:, :S], ALU.mult, ALU.add
+            )
+        quantize(w4_mx, 0, N)
+        z2_mx = mx_tiles("z2", S)
+        interleave("vector", z2_mx[0], z2_planes)
+        quantize(z2_mx, 0, S)
+        for t in planes:
+            product(h_ps[t], w4_mx, t, z2_mx[1], z2_mx[2], False, True)
+
+        out_rows = out.rearrange("(p t) s -> p t s", t=PACK)
+        gate = sb.tile([P, PACK, S], F32, name="gate")
+        res = [sb.tile([P, S], F32, name="res%d" % t) for t in planes]
+
+        def fetch_h(t):
+            nc.vector.tensor_copy(y_win[t][:, :S], h_ps[t][:])
+            nc.scalar.activation(d_win[t][:, S:], y_win[t][:].indirect(n4_t[:]), ACT.Copy)
+
+        def fetch_gate(t):
+            nc.vector.tensor_tensor(d_win[t][:, :S], d_win[t][:, S:], h_ps[t][:], ALU.subtract)
+            nc.scalar.activation(gate[:, t, :], d_win[t][:].indirect(n5_t[:]), ACT.Sigmoid)
+
+        def store(t):
+            nc.vector.tensor_tensor(res[t][:], gate[:, t, :], h_ps[t][:], ALU.mult)
+            nc.sync.dma_start(out_rows[:, t, :], res[t][:])
+
+        for step in range(PACK + 2):
+            if step < PACK:
+                fetch_h(step)
+            if 0 <= step - 1 < PACK:
+                fetch_gate(step - 1)
+            if 0 <= step - 2 < PACK:
+                store(step - 2)

@@ -33,21 +33,24 @@ def tile_picked_hjoinepkehphopd_none_p_kernel(
             nc.sync.dma_start(tile[:], src)
             return tile
 
-        def load_part(name, w, u):
+        def load_part(raw, w, u):
             width = w.shape[1] // 2
-            raw = sb.tile([P, PACK, width], F32, name="%s_raw%d" % (name, u))
-            nc.sync.dma_start(raw[:], w[:, u * width : (u + 1) * width].rearrange("(p j) c -> p j c", j=PACK))
+            nc.sync.dma_start(raw, w[:, u * width : (u + 1) * width].rearrange("(p j) c -> p j c", j=PACK))
             return raw
 
+        def half_tile(name):
+            raw = sb.tile([P, PACK, H // 2], F32, name=name, tag=name)
+            return raw[:]
+
         def load_gain(queue, name, v):
-            tile = sb.tile([P, PACK], F32, name=name)
+            tile = sb.tile([P, PACK], F32, name=name, tag=name, align_bytes=64)
             queue.dma_start(tile[:], v.rearrange("(p t) o -> p (t o)", t=PACK))
             return tile
 
-        def deal(engine, grouped, raw, u):
+        def deal(engine, grouped, raw, c0):
             ms = raw.shape[2] // PACK
-            dst = grouped[:].rearrange("p (t m j) -> p m j t", t=PACK, j=PACK)[:, u * ms : (u + 1) * ms]
-            src = raw[:].rearrange("p j (m t) -> p m j t", t=PACK)
+            dst = grouped[:].rearrange("p (t m j) -> p m j t", t=PACK, j=PACK)[:, c0 // PACK : c0 // PACK + ms]
+            src = raw.rearrange("p j (m t) -> p m j t", t=PACK)
             if engine == "gpsimd":
                 dst = dst.rearrange("p m j t -> p m t j")
                 src = src.rearrange("p m j t -> p m t j")
@@ -57,8 +60,8 @@ def tile_picked_hjoinepkehphopd_none_p_kernel(
             else:
                 nc.vector.tensor_copy(dst, src)
 
-        def mx_tiles(name, cols):
-            grouped = sb.tile([P, PACK * cols], BF16, name=name + "_bf16", align_bytes=64)
+        def mx_tiles(name, cols, tag):
+            grouped = sb.tile([P, PACK * cols], BF16, name=name + "_bf16", tag=tag, align_bytes=64)
             codes = sb.tile([P, cols], U32, name=name + "_codes", align_bytes=64)
             scales = sb.tile([P, cols], U8, name=name + "_scales", align_bytes=64)
             return grouped, codes, scales
@@ -91,28 +94,28 @@ def tile_picked_hjoinepkehphopd_none_p_kernel(
 
         xs = sb.tile([P, T], U8, name="xs")
         nc.vector.memset(xs[:].bitcast(I32), 0)
-        w1_raw = [load_part("w1", w1, 0)]
         offs_t = load_list("offs_t", offs)
         hz_t = load_list("hz_t", hz)
-        n1_t = load_list("n1_t", n1)
-        n2_t = load_list("n2_t", n2)
-        n3_t = load_list("n3_t", n3)
-        n4_t = load_list("n4_t", n4)
-        w1_raw.append(load_part("w1", w1, 1))
+        w1_raw = sb.tile([P, PACK, H], F32, name="w1_raw")
+        nc.sync.dma_start(w1_raw[:], w1.rearrange("(p j) c -> p j c", j=PACK))
+        for r in range(4):
+            nc.sync.dma_start(xs[r:P:32, :].bitcast(I32), x_scales[0][r:16:4, :].bitcast(I32))
+        for r in (2, 3):
+            nc.sync.dma_start(xs[14 + r : P : 32, :].bitcast(I32), x_scales[0][r:16:4, :].bitcast(I32))
         xw = sb.tile([P, T], I32, name="xw")
         nc.sync.dma_start(xw[:], x_words[0].rearrange("p c r -> p (c r)").bitcast(I32))
-        for r in range(4):
-            nc.scalar.dma_start(xs[r:P:32, :].bitcast(I32), x_scales[0][r:16:4, :].bitcast(I32))
-        for r in (2, 3):
-            nc.scalar.dma_start(xs[14 + r : P : 32, :].bitcast(I32), x_scales[0][r:16:4, :].bitcast(I32))
         tau_t = load_gain(nc.gpsimd, "tau_t", tau)
         gn_t = load_gain(nc.gpsimd, "gn_t", gn)
-        w2_raw = [load_part("w2", w2, u) for u in range(2)]
         sl_t = load_gain(nc.sync, "sl_t", sl)
         th_t = load_gain(nc.sync, "th_t", th)
+        n1_t = load_list("n1_t", n1)
+        w2_raw = [load_part(half_tile("w2_%d" % u), w2, u) for u in range(2)]
+        n2_t = load_list("n2_t", n2)
+        w3_raw = [load_part(half_tile("w3_%d" % u), w3, u) for u in range(2)]
         gm_t = load_gain(nc.sync, "gm_t", gm)
-        w3_raw = [load_part("w3", w3, u) for u in range(2)]
-        w4_raw = [load_part("w4", w4, u) for u in range(2)]
+        n3_t = load_list("n3_t", n3)
+        w4_raw = [load_part(half_tile("w4_%d" % u), w4, u) for u in range(2)]
+        n4_t = load_list("n4_t", n4)
         n5_t = load_list("n5_t", n5)
 
         y_win = [sb.tile([P, 2 * S], F32, name="y_win%d" % t) for t in planes]
@@ -121,22 +124,28 @@ def tile_picked_hjoinepkehphopd_none_p_kernel(
         for t in planes:
             nc.vector.memset(y_win[t][:, S:], 0.0)
 
-        w1_mx = mx_tiles("w1", H)
-        for u in range(2):
-            deal("vector", w1_mx[0], w1_raw[u], u)
-        xq_scales = sb.tile([P, S], U8, name="xq_scales", align_bytes=64)
-        nc.vector.tensor_copy(xq_scales[:], xs[:].indirect(offs_t[:]))
-        quantize(w1_mx, 0, H)
+        ntau = sb.tile([P, PACK], F32, name="ntau")
+        nc.gpsimd.tensor_scalar(ntau[:], tau_t[:], -1.0, 0.0, ALU.mult, ALU.add)
+        gn2_lo = sb.tile([P, 2], F32, name="gn2_lo")
+        nc.gpsimd.tensor_scalar(gn2_lo[:], gn_t[:, :2], 2.0, 0.0, ALU.mult, ALU.add)
+        gn2 = [gn2_lo[:, 0:1], gn2_lo[:, 1:2]]
+        nsl = sb.tile([P, PACK], F32, name="nsl")
+        nc.gpsimd.tensor_scalar(nsl[:], sl_t[:], -1.0, 0.0, ALU.mult, ALU.add)
+        sg_bias = sb.tile([P, PACK], F32, name="sg_bias")
+        nc.gpsimd.tensor_tensor(sg_bias[:], nsl[:], th_t[:], ALU.mult)
+
+        w1_mx = mx_tiles("w1", H, "slot_c")
+        deal("vector", w1_mx[0], w1_raw[:, :, :256], 0)
+        deal("scalar", w1_mx[0], w1_raw[:, :, 256:], 256)
         xh_picked = sb.tile([P, S], U8, name="xh_picked", align_bytes=64)
         nc.vector.tensor_copy(xh_picked[:], xs[:].indirect(hz_t[:]))
         xh_scales = sb.tile([P, S], U8, name="xh_scales", align_bytes=64)
         nc.vector.tensor_copy(xh_scales[:].bitcast(I32), xh_picked[:].bitcast(I32))
         for r in (2, 3):
-            nc.gpsimd.dma_start(xh_scales[r:P:32, :].bitcast(I32), xh_picked[14 + r : P : 32, :].bitcast(I32))
-        ntau = sb.tile([P, PACK], F32, name="ntau")
-        nc.vector.tensor_scalar(ntau[:], tau_t[:], -1.0, None, ALU.mult)
-        gn2 = sb.tile([P, PACK], F32, name="gn2")
-        nc.vector.tensor_scalar(gn2[:], gn_t[:], 2.0, None, ALU.mult)
+            nc.scalar.dma_start(xh_scales[r:P:32, :].bitcast(I32), xh_picked[14 + r : P : 32, :].bitcast(I32))
+        xq_scales = sb.tile([P, S], U8, name="xq_scales", align_bytes=64)
+        nc.vector.tensor_copy(xq_scales[:], xs[:].indirect(offs_t[:]))
+        quantize(w1_mx, 0, H)
 
         xq_words = sb.tile([P, S], U32, name="xq_words", align_bytes=64)
         nc.vector.tensor_copy(xq_words[:], xw[:].bitcast(U32).indirect(offs_t[:]))
@@ -145,33 +154,34 @@ def tile_picked_hjoinepkehphopd_none_p_kernel(
             product(y_ps[t], w1_mx, t, xq_words, xq_scales, True, True)
         xh_words = sb.tile([P, S], U32, name="xh_words", align_bytes=64)
         nc.vector.tensor_copy(xh_words[:], xw[:].bitcast(U32).indirect(hz_t[:]))
-        w2_mx = mx_tiles("w2", H)
+        w2_mx = mx_tiles("w2", H, "slot_f")
         for u in range(2):
-            deal("gpsimd", w2_mx[0], w2_raw[u], u)
-        top = [sb.tile([P, 1], F32, name="top%d" % t) for t in planes]
+            deal("gpsimd", w2_mx[0], w2_raw[u], 256 * u)
+        top = [sb.tile([P, 1], F32, name="top%d" % t, tag="top%d" % t) for t in planes]
         ea_bias = [sb.tile([P, 1], F32, name="ea_bias%d" % t) for t in planes]
         for t in planes:
             nc.vector.tensor_scalar(y_win[t][:, :S], y_ps[t][:], 1.0, None, ALU.mult, ALU.max, accum_out=top[t][:])
-            nc.vector.tensor_scalar(ea_bias[t][:], top[t][:], ntau[:, t : t + 1], None, ALU.mult)
+
+        def make_bias(t):
+            nc.scalar.activation(ea_bias[t][:], top[t][:], ACT.Copy, scale=ntau[:, t : t + 1])
+
+        make_bias(0)
+        for t in planes:
+            if t == 1:
+                make_bias(1)
+            if 1 <= t < PACK - 1:
+                make_bias(t + 1)
             nc.scalar.activation(
                 d_win[t][:, S:], y_win[t][:].indirect(n1_t[:]), ACT.Exp, bias=ea_bias[t][:], scale=tau_t[:, t : t + 1]
             )
         z_planes = sb.tile([P, PACK, S], F32, name="z_planes")
-        for t in planes:
+
+        def make_z(t):
             nc.vector.scalar_tensor_tensor(
-                z_planes[:, t, :], y_ps[t][:], gn2[:, t : t + 1], d_win[t][:, S:], ALU.mult, ALU.mult
+                z_planes[:, t, :], y_ps[t][:], gn2[t], d_win[t][:, S:], ALU.mult, ALU.mult
             )
 
-        sg_bias = sb.tile([P, PACK], F32, name="sg_bias")
-        nc.vector.scalar_tensor_tensor(sg_bias[:], sl_t[:], -1.0, th_t[:], ALU.mult, ALU.mult)
-        d_ps = [psum.tile([P, S], F32, name="d_ps%d" % t, tag="bank%d" % (PACK + t)) for t in planes]
-        for t in planes:
-            quantize(w2_mx, t * P, (t + 1) * P)
-            product(d_ps[t], w2_mx, t, xh_words, xh_scales, True, True)
-        w3_mx = mx_tiles("w3", N)
-        for u in range(2):
-            deal("gpsimd", w3_mx[0], w3_raw[u], u)
-        for t in planes:
+        def make_sg(t):
             nc.vector.tensor_copy(d_win[t][:, :S], d_ps[t][:])
             nc.scalar.activation(
                 st_win[t][:, S:],
@@ -180,37 +190,68 @@ def tile_picked_hjoinepkehphopd_none_p_kernel(
                 bias=sg_bias[:, t : t + 1],
                 scale=sl_t[:, t : t + 1],
             )
-        z_mx = mx_tiles("z", S)
-        interleave("vector", z_mx[0], z_planes)
+
+        make_z(0)
+        make_z(1)
+        gn2_hi = sb.tile([P, 2], F32, name="gn2_hi", tag="w2_1")
+        nc.vector.tensor_scalar(gn2_hi[:], gn_t[:, 2:], 2.0, None, ALU.mult)
+        gn2.extend([gn2_hi[:, 0:1], gn2_hi[:, 1:2]])
+        d_ps = [psum.tile([P, S], F32, name="d_ps%d" % t, tag="bank%d" % (PACK + t)) for t in planes]
+        for t in planes:
+            quantize(w2_mx, t * P, (t + 1) * P)
+            product(d_ps[t], w2_mx, t, xh_words, xh_scales, True, True)
+        w3_mx = mx_tiles("w3", N, "slot_f")
+        for u in range(2):
+            deal("gpsimd", w3_mx[0], w3_raw[u], 256 * u)
+        make_z(2)
+        make_sg(0)
+        make_z(3)
+        for t in range(1, PACK):
+            make_sg(t)
         far = sb.tile([P, PACK, S], F32, name="far")
         z2_planes = sb.tile([P, PACK, S], F32, name="z2_planes")
-        for t in planes:
+
+        def make_st(t):
             nc.vector.scalar_tensor_tensor(
                 st_win[t][:, :S], d_ps[t][:], gm_t[:, t : t + 1], st_win[t][:, S:], ALU.mult, ALU.mult
             )
             nc.scalar.activation(far[:, t, :], st_win[t][:].indirect(n3_t[:]), ACT.Copy)
+
+        def make_z2(t):
+            nc.vector.scalar_tensor_tensor(
+                z2_planes[:, t, :], far[:, t, :], -0.5, st_win[t][:, :S], ALU.mult, ALU.add
+            )
+
+        z_mx = mx_tiles("z", S, "z_bf16")
+        make_st(0)
+        interleave("vector", z_mx[0], z_planes)
+        make_st(1)
         quantize(z_mx, 0, S)
+        make_st(2)
+        make_st(3)
+        w4_mx = mx_tiles("w4", N, "gm_t")
+        deal("vector", w4_mx[0], w4_raw[0], 0)
+        deal("vector", w4_mx[0], w4_raw[1][:, :, :128], 256)
+        deal("scalar", w4_mx[0], w4_raw[1][:, :, 128:], 384)
         quantize(w3_mx, 0, N)
         h_ps = [psum.tile([P, S], F32, name="h_ps%d" % t, tag="bank%d" % t) for t in planes]
         for t in planes:
             product(h_ps[t], w3_mx, t, z_mx[1], z_mx[2], True, False)
-        w4_mx = mx_tiles("w4", N)
-        for u in range(2):
-            deal("vector", w4_mx[0], w4_raw[u], u)
         for t in planes:
-            nc.vector.scalar_tensor_tensor(
-                z2_planes[:, t, :], far[:, t, :], -0.5, st_win[t][:, :S], ALU.mult, ALU.add
-            )
-        quantize(w4_mx, 0, N)
-        z2_mx = mx_tiles("z2", S)
+            make_z2(t)
+        z2_mx = mx_tiles("z2", S, "z2_bf16")
         interleave("vector", z2_mx[0], z2_planes)
+        quantize(w4_mx, 0, P)
         quantize(z2_mx, 0, S)
-        for t in planes:
-            product(h_ps[t], w4_mx, t, z2_mx[1], z2_mx[2], False, True)
 
         out_rows = out.rearrange("(p t) s -> p t s", t=PACK)
         gate = sb.tile([P, PACK, S], F32, name="gate")
         res = [sb.tile([P, S], F32, name="res%d" % t) for t in planes]
+
+        def close_h(t):
+            if t > 0:
+                quantize(w4_mx, t * P, (t + 1) * P)
+            product(h_ps[t], w4_mx, t, z2_mx[1], z2_mx[2], False, True)
 
         def fetch_h(t):
             nc.vector.tensor_copy(y_win[t][:, :S], h_ps[t][:])
@@ -224,7 +265,10 @@ def tile_picked_hjoinepkehphopd_none_p_kernel(
             nc.vector.tensor_tensor(res[t][:], gate[:, t, :], h_ps[t][:], ALU.mult)
             nc.sync.dma_start(out_rows[:, t, :], res[t][:])
 
+        close_h(0)
         for step in range(PACK + 2):
+            if step + 1 < PACK:
+                close_h(step + 1)
             if step < PACK:
                 fetch_h(step)
             if 0 <= step - 1 < PACK:

@@ -49,11 +49,9 @@ def tile_picked_hjoinepkehphopd_none_p_kernel(
 
         def deal(engine, grouped, raw, c0):
             ms = raw.shape[2] // PACK
-            dst = grouped[:].rearrange("p (t m j) -> p m j t", t=PACK, j=PACK)[:, c0 // PACK : c0 // PACK + ms]
-            src = raw.rearrange("p j (m t) -> p m j t", t=PACK)
+            dst = grouped[:].rearrange("p (t m j) -> p m t j", t=PACK, j=PACK)[:, c0 // PACK : c0 // PACK + ms]
+            src = raw.rearrange("p j (m t) -> p m t j", t=PACK)
             if engine == "gpsimd":
-                dst = dst.rearrange("p m j t -> p m t j")
-                src = src.rearrange("p m j t -> p m t j")
                 nc.gpsimd.tensor_scalar(dst, src, 1.0, 0.0, ALU.mult, ALU.add)
             elif engine == "scalar":
                 nc.scalar.copy(dst, src)
@@ -91,6 +89,7 @@ def tile_picked_hjoinepkehphopd_none_p_kernel(
                 nc.vector.tensor_copy(dst, src)
 
         planes = range(PACK)
+        halves = [slice(0, S // 2), slice(S // 2, S)]
 
         xs = sb.tile([P, T], U8, name="xs")
         nc.vector.memset(xs[:].bitcast(I32), 0)
@@ -126,9 +125,8 @@ def tile_picked_hjoinepkehphopd_none_p_kernel(
 
         ntau = sb.tile([P, PACK], F32, name="ntau")
         nc.gpsimd.tensor_scalar(ntau[:], tau_t[:], -1.0, 0.0, ALU.mult, ALU.add)
-        gn2_lo = sb.tile([P, 2], F32, name="gn2_lo")
-        nc.gpsimd.tensor_scalar(gn2_lo[:], gn_t[:, :2], 2.0, 0.0, ALU.mult, ALU.add)
-        gn2 = [gn2_lo[:, 0:1], gn2_lo[:, 1:2]]
+        gn2 = sb.tile([P, PACK], F32, name="gn2")
+        nc.gpsimd.tensor_scalar(gn2[:], gn_t[:], 2.0, 0.0, ALU.mult, ALU.add)
         nsl = sb.tile([P, PACK], F32, name="nsl")
         nc.gpsimd.tensor_scalar(nsl[:], sl_t[:], -1.0, 0.0, ALU.mult, ALU.add)
         sg_bias = sb.tile([P, PACK], F32, name="sg_bias")
@@ -155,8 +153,7 @@ def tile_picked_hjoinepkehphopd_none_p_kernel(
         xh_words = sb.tile([P, S], U32, name="xh_words", align_bytes=64)
         nc.vector.tensor_copy(xh_words[:], xw[:].bitcast(U32).indirect(hz_t[:]))
         w2_mx = mx_tiles("w2", H, "slot_f")
-        for u in range(2):
-            deal("gpsimd", w2_mx[0], w2_raw[u], 256 * u)
+        deal("gpsimd", w2_mx[0], w2_raw[0], 0)
         top = [sb.tile([P, 1], F32, name="top%d" % t, tag="top%d" % t) for t in planes]
         ea_bias = [sb.tile([P, 1], F32, name="ea_bias%d" % t) for t in planes]
         for t in planes:
@@ -174,11 +171,10 @@ def tile_picked_hjoinepkehphopd_none_p_kernel(
             nc.scalar.activation(
                 d_win[t][:, S:], y_win[t][:].indirect(n1_t[:]), ACT.Exp, bias=ea_bias[t][:], scale=tau_t[:, t : t + 1]
             )
-        z_planes = sb.tile([P, PACK, S], F32, name="z_planes")
 
         def make_z(t):
             nc.vector.scalar_tensor_tensor(
-                z_planes[:, t, :], y_ps[t][:], gn2[t], d_win[t][:, S:], ALU.mult, ALU.mult
+                z_planes[:, t, :], y_ps[t][:], gn2[:, t : t + 1], d_win[t][:, S:], ALU.mult, ALU.mult
             )
 
         def make_sg(t):
@@ -191,11 +187,8 @@ def tile_picked_hjoinepkehphopd_none_p_kernel(
                 scale=sl_t[:, t : t + 1],
             )
 
-        make_z(0)
-        make_z(1)
-        gn2_hi = sb.tile([P, 2], F32, name="gn2_hi", tag="w2_1")
-        nc.vector.tensor_scalar(gn2_hi[:], gn_t[:, 2:], 2.0, None, ALU.mult)
-        gn2.extend([gn2_hi[:, 0:1], gn2_hi[:, 1:2]])
+        deal("vector", w2_mx[0], w2_raw[1], 256)
+        z_planes = sb.tile([P, PACK, S], F32, name="z_planes", tag="w2_1")
         d_ps = [psum.tile([P, S], F32, name="d_ps%d" % t, tag="bank%d" % (PACK + t)) for t in planes]
         for t in planes:
             quantize(w2_mx, t * P, (t + 1) * P)
@@ -203,10 +196,8 @@ def tile_picked_hjoinepkehphopd_none_p_kernel(
         w3_mx = mx_tiles("w3", N, "slot_f")
         for u in range(2):
             deal("gpsimd", w3_mx[0], w3_raw[u], 256 * u)
-        make_z(2)
-        make_sg(0)
-        make_z(3)
-        for t in range(1, PACK):
+        for t in planes:
+            make_z(t)
             make_sg(t)
         far = sb.tile([P, PACK, S], F32, name="far")
         z2_planes = sb.tile([P, PACK, S], F32, name="z2_planes")
@@ -231,8 +222,7 @@ def tile_picked_hjoinepkehphopd_none_p_kernel(
         make_st(3)
         w4_mx = mx_tiles("w4", N, "gm_t")
         deal("vector", w4_mx[0], w4_raw[0], 0)
-        deal("vector", w4_mx[0], w4_raw[1][:, :, :128], 256)
-        deal("scalar", w4_mx[0], w4_raw[1][:, :, 128:], 384)
+        deal("scalar", w4_mx[0], w4_raw[1], 256)
         quantize(w3_mx, 0, N)
         h_ps = [psum.tile([P, S], F32, name="h_ps%d" % t, tag="bank%d" % t) for t in planes]
         for t in planes:
@@ -259,11 +249,14 @@ def tile_picked_hjoinepkehphopd_none_p_kernel(
 
         def fetch_gate(t):
             nc.vector.tensor_tensor(d_win[t][:, :S], d_win[t][:, S:], h_ps[t][:], ALU.subtract)
-            nc.scalar.activation(gate[:, t, :], d_win[t][:].indirect(n5_t[:]), ACT.Sigmoid)
+            for places in halves if t == PACK - 1 else [slice(0, S)]:
+                entries = n5_t[:, places.start // 16 : places.stop // 16]
+                nc.scalar.activation(gate[:, t, places], d_win[t][:].indirect(entries), ACT.Sigmoid)
 
         def store(t):
-            nc.vector.tensor_tensor(res[t][:], gate[:, t, :], h_ps[t][:], ALU.mult)
-            nc.sync.dma_start(out_rows[:, t, :], res[t][:])
+            for places in halves if t == PACK - 1 else [slice(0, S)]:
+                nc.vector.tensor_tensor(res[t][:, places], gate[:, t, places], h_ps[t][:, places], ALU.mult)
+                nc.sync.dma_start(out_rows[:, t, places], res[t][:, places])
 
         close_h(0)
         for step in range(PACK + 2):

@@ -105,10 +105,11 @@ def tile_picked_hjoinepkehphopd_none_p_kernel(
         nc.sync.dma_start(xw[:], x_words[0].rearrange("p c r -> p (c r)").bitcast(I32))
         tau_t = load_gain(nc.gpsimd, "tau_t", tau)
         gn_t = load_gain(nc.gpsimd, "gn_t", gn)
-        sl_t = load_gain(nc.sync, "sl_t", sl)
-        th_t = load_gain(nc.sync, "th_t", th)
+        sl_t = load_gain(nc.gpsimd, "sl_t", sl)
+        th_t = load_gain(nc.gpsimd, "th_t", th)
+        w2_raw = [load_part(half_tile("w2_0"), w2, 0)]
         n1_t = load_list("n1_t", n1)
-        w2_raw = [load_part(half_tile("w2_%d" % u), w2, u) for u in range(2)]
+        w2_raw.append(load_part(half_tile("w2_1"), w2, 1))
         n2_t = load_list("n2_t", n2)
         w3_raw = [load_part(half_tile("w3_%d" % u), w3, u) for u in range(2)]
         gm_t = load_gain(nc.sync, "gm_t", gm)

from contextlib import ExitStack

import concourse.mybir as mybir

K, T, S, N, H = 512, 2048, 256, 512, 512
FLOPS = 4 * 2 * 512 * 512 * 256

F32 = mybir.dt.float32
BF16 = mybir.dt.bfloat16
I32 = mybir.dt.int32
U32 = mybir.dt.uint32
U16 = mybir.dt.uint16
U8 = mybir.dt.uint8
FP8X4 = mybir.dt.float8_e4m3fn_x4
ALU = mybir.AluOpType
ACT = mybir.ActivationFunctionType

P = 128
PACK = 4


def tile_picked_hjoinepkehphopd_none_p_kernel(
    tc, x_words, x_scales, w1, w2, tau, sl, th, gn, gm, w3, w4, offs, hz, n1, n2, n3, n4, n5, out
):
    nc = tc.nc
    with ExitStack() as ctx:
        lists = ctx.enter_context(tc.tile_pool(name="lists", bufs=1))
        sb = ctx.enter_context(tc.tile_pool(name="sb", bufs=1))
        psum = ctx.enter_context(tc.psum_pool(name="psum", bufs=1))

        def load_list(name, src):
            tile = lists.tile([P, S // 16], U16, name=name)
            nc.sync.dma_start(tile[:], src)
            return tile

        def load_part(raw, w, u):
            width = w.shape[1] // 2
            nc.sync.dma_start(raw, w[:, u * width : (u + 1) * width].rearrange("(p j) c -> p j c", j=PACK))
            return raw

        def half_tile(name):
            raw = sb.tile([P, PACK, H // 2], F32, name=name, tag=name)
            return raw[:]

        def load_gain(queue, name, v):
            tile = sb.tile([P, PACK], F32, name=name, tag=name, align_bytes=64)
            queue.dma_start(tile[:], v.rearrange("(p t) o -> p (t o)", t=PACK))
            return tile

        def deal(engine, grouped, raw, c0):
            ms = raw.shape[2] // PACK
            dst = grouped[:].rearrange("p (t m j) -> p m t j", t=PACK, j=PACK)[:, c0 // PACK : c0 // PACK + ms]
            src = raw.rearrange("p j (m t) -> p m t j", t=PACK)
            if engine == "gpsimd":
                nc.gpsimd.tensor_scalar(dst, src, 1.0, 0.0, ALU.mult, ALU.add)
            elif engine == "scalar":
                nc.scalar.copy(dst, src)
            else:
                nc.vector.tensor_copy(dst, src)

        def mx_tiles(name, cols, tag):
            grouped = sb.tile([P, PACK * cols], BF16, name=name + "_bf16", tag=tag, align_bytes=64)
            codes = sb.tile([P, cols], U32, name=name + "_codes", align_bytes=64)
            scales = sb.tile([P, cols], U8, name=name + "_scales", align_bytes=64)
            return grouped, codes, scales

        def quantize(tiles, c0, c1):
            grouped, codes, scales = tiles
            nc.vector.quantize_mx(codes[:, c0:c1].bitcast(FP8X4), scales[:, c0:c1], grouped[:, PACK * c0 : PACK * c1])

        def product(acc, w_tiles, t, codes, scales, start, stop):
            cols = slice(t * P, (t + 1) * P)
            nc.tensor.matmul_mx(
                out=acc[:],
                lhsT=w_tiles[1][:, cols].bitcast(FP8X4),
                lhsT_scale=w_tiles[2][:, cols],
                rhs=codes[:].bitcast(FP8X4),
                rhs_scale=scales[:],
                start=start,
                stop=stop,
            )

        def interleave(engine, grouped, planes):
            dst = grouped[:].rearrange("p (c i t) -> p c t i", t=PACK, i=4)
            src = planes[:].rearrange("p t (c i) -> p c t i", i=4)
            if engine == "scalar":
                nc.scalar.copy(dst, src)
            else:
                nc.vector.tensor_copy(dst, src)

        planes = range(PACK)
        halves = [slice(0, S // 2), slice(S // 2, S)]

        xs = sb.tile([P, T], U8, name="xs")
        nc.vector.memset(xs[:].bitcast(I32), 0)
        offs_t = load_list("offs_t", offs)
        hz_t = load_list("hz_t", hz)
        w1_raw = sb.tile([P, PACK, H], F32, name="w1_raw")
        nc.sync.dma_start(w1_raw[:], w1.rearrange("(p j) c -> p j c", j=PACK))
        for r in range(4):
            nc.sync.dma_start(xs[r:P:32, :].bitcast(I32), x_scales[0][r:16:4, :].bitcast(I32))
        for r in (2, 3):
            nc.sync.dma_start(xs[14 + r : P : 32, :].bitcast(I32), x_scales[0][r:16:4, :].bitcast(I32))
        xw = sb.tile([P, T], I32, name="xw")
        nc.sync.dma_start(xw[:], x_words[0].rearrange("p c r -> p (c r)").bitcast(I32))
        tau_t = load_gain(nc.gpsimd, "tau_t", tau)
        gn_t = load_gain(nc.gpsimd, "gn_t", gn)
        sl_t = load_gain(nc.gpsimd, "sl_t", sl)
        th_t = load_gain(nc.gpsimd, "th_t", th)
        w2_raw = [load_part(half_tile("w2_0"), w2, 0)]
        n1_t = load_list("n1_t", n1)
        w2_raw.append(load_part(half_tile("w2_1"), w2, 1))
        n2_t = load_list("n2_t", n2)
        w3_raw = [load_part(half_tile("w3_%d" % u), w3, u) for u in range(2)]
        gm_t = load_gain(nc.sync, "gm_t", gm)
        n3_t = load_list("n3_t", n3)
        w4_raw = [load_part(half_tile("w4_%d" % u), w4, u) for u in range(2)]
        n4_t = load_list("n4_t", n4)
        n5_t = load_list("n5_t", n5)

        y_win = [sb.tile([P, 2 * S], F32, name="y_win%d" % t) for t in planes]
        d_win = [sb.tile([P, 2 * S], F32, name="d_win%d" % t) for t in planes]
        st_win = [sb.tile([P, 2 * S], F32, name="st_win%d" % t) for t in planes]
        for t in planes:
            nc.vector.memset(y_win[t][:, S:], 0.0)

        ntau = sb.tile([P, PACK], F32, name="ntau")
        nc.gpsimd.tensor_scalar(ntau[:], tau_t[:], -1.0, 0.0, ALU.mult, ALU.add)
        gn2 = sb.tile([P, PACK], F32, name="gn2")
        nc.gpsimd.tensor_scalar(gn2[:], gn_t[:], 2.0, 0.0, ALU.mult, ALU.add)
        nsl = sb.tile([P, PACK], F32, name="nsl")
        nc.gpsimd.tensor_scalar(nsl[:], sl_t[:], -1.0, 0.0, ALU.mult, ALU.add)
        sg_bias = sb.tile([P, PACK], F32, name="sg_bias")
        nc.gpsimd.tensor_tensor(sg_bias[:], nsl[:], th_t[:], ALU.mult)

        w1_mx = mx_tiles("w1", H, "slot_c")
        deal("vector", w1_mx[0], w1_raw[:, :, :256], 0)
        deal("scalar", w1_mx[0], w1_raw[:, :, 256:], 256)
        xh_picked = sb.tile([P, S], U8, name="xh_picked", align_bytes=64)
        nc.vector.tensor_copy(xh_picked[:], xs[:].indirect(hz_t[:]))
        xh_scales = sb.tile([P, S], U8, name="xh_scales", align_bytes=64)
        nc.vector.tensor_copy(xh_scales[:].bitcast(I32), xh_picked[:].bitcast(I32))
        for r in (2, 3):
            nc.scalar.dma_start(xh_scales[r:P:32, :].bitcast(I32), xh_picked[14 + r : P : 32, :].bitcast(I32))
        xq_scales = sb.tile([P, S], U8, name="xq_scales", align_bytes=64)
        nc.vector.tensor_copy(xq_scales[:], xs[:].indirect(offs_t[:]))
        quantize(w1_mx, 0, H)

        xq_words = sb.tile([P, S], U32, name="xq_words", align_bytes=64)
        nc.vector.tensor_copy(xq_words[:], xw[:].bitcast(U32).indirect(offs_t[:]))
        y_ps = [psum.tile([P, S], F32, name="y_ps%d" % t, tag="bank%d" % t) for t in planes]
        for t in planes:
            product(y_ps[t], w1_mx, t, xq_words, xq_scales, True, True)
        xh_words = sb.tile([P, S], U32, name="xh_words", align_bytes=64)
        nc.vector.tensor_copy(xh_words[:], xw[:].bitcast(U32).indirect(hz_t[:]))
        w2_mx = mx_tiles("w2", H, "slot_f")
        deal("gpsimd", w2_mx[0], w2_raw[0], 0)
        top = [sb.tile([P, 1], F32, name="top%d" % t, tag="top%d" % t) for t in planes]
        ea_bias = [sb.tile([P, 1], F32, name="ea_bias%d" % t) for t in planes]
        for t in planes:
            nc.vector.tensor_scalar(y_win[t][:, :S], y_ps[t][:], 1.0, None, ALU.mult, ALU.max, accum_out=top[t][:])

        def make_bias(t):
            nc.scalar.activation(ea_bias[t][:], top[t][:], ACT.Copy, scale=ntau[:, t : t + 1])

        make_bias(0)
        for t in planes:
            if t == 1:
                make_bias(1)
            if 1 <= t < PACK - 1:
                make_bias(t + 1)
            nc.scalar.activation(
                d_win[t][:, S:], y_win[t][:].indirect(n1_t[:]), ACT.Exp, bias=ea_bias[t][:], scale=tau_t[:, t : t + 1]
            )

        def make_z(t):
            nc.vector.scalar_tensor_tensor(
                z_planes[:, t, :], y_ps[t][:], gn2[:, t : t + 1], d_win[t][:, S:], ALU.mult, ALU.mult
            )

        def make_sg(t):
            nc.vector.tensor_copy(d_win[t][:, :S], d_ps[t][:])
            nc.scalar.activation(
                st_win[t][:, S:],
                d_win[t][:].indirect(n2_t[:]),
                ACT.Sigmoid,
                bias=sg_bias[:, t : t + 1],
                scale=sl_t[:, t : t + 1],
            )

        deal("vector", w2_mx[0], w2_raw[1], 256)
        z_planes = sb.tile([P, PACK, S], F32, name="z_planes", tag="w2_1")
        d_ps = [psum.tile([P, S], F32, name="d_ps%d" % t, tag="bank%d" % (PACK + t)) for t in planes]
        for t in planes:
            quantize(w2_mx, t * P, (t + 1) * P)
            product(d_ps[t], w2_mx, t, xh_words, xh_scales, True, True)
        w3_mx = mx_tiles("w3", N, "slot_f")
        for u in range(2):
            deal("gpsimd", w3_mx[0], w3_raw[u], 256 * u)
        for t in planes:
            make_z(t)
            make_sg(t)
        far = sb.tile([P, PACK, S], F32, name="far")
        z2_planes = sb.tile([P, PACK, S], F32, name="z2_planes")

        def make_st(t):
            nc.vector.scalar_tensor_tensor(
                st_win[t][:, :S], d_ps[t][:], gm_t[:, t : t + 1], st_win[t][:, S:], ALU.mult, ALU.mult
            )
            nc.scalar.activation(far[:, t, :], st_win[t][:].indirect(n3_t[:]), ACT.Copy)

        def make_z2(t):
            nc.vector.scalar_tensor_tensor(
                z2_planes[:, t, :], far[:, t, :], -0.5, st_win[t][:, :S], ALU.mult, ALU.add
            )

        z_mx = mx_tiles("z", S, "z_bf16")
        make_st(0)
        interleave("vector", z_mx[0], z_planes)
        make_st(1)
        quantize(z_mx, 0, S)
        make_st(2)
        make_st(3)
        w4_mx = mx_tiles("w4", N, "gm_t")
        deal("vector", w4_mx[0], w4_raw[0], 0)
        deal("scalar", w4_mx[0], w4_raw[1], 256)
        quantize(w3_mx, 0, N)
        h_ps = [psum.tile([P, S], F32, name="h_ps%d" % t, tag="bank%d" % t) for t in planes]
        for t in planes:
            product(h_ps[t], w3_mx, t, z_mx[1], z_mx[2], True, False)
        for t in planes:
            make_z2(t)
        z2_mx = mx_tiles("z2", S, "z2_bf16")
        interleave("vector", z2_mx[0], z2_planes)
        quantize(w4_mx, 0, P)
        quantize(z2_mx, 0, S)

        out_rows = out.rearrange("(p t) s -> p t s", t=PACK)
        gate = sb.tile([P, PACK, S], F32, name="gate")
        res = [sb.tile([P, S], F32, name="res%d" % t) for t in planes]

        def close_h(t):
            if t > 0:
                quantize(w4_mx, t * P, (t + 1) * P)
            product(h_ps[t], w4_mx, t, z2_mx[1], z2_mx[2], False, True)

        def fetch_h(t):
            nc.vector.tensor_copy(y_win[t][:, :S], h_ps[t][:])
            nc.scalar.activation(d_win[t][:, S:], y_win[t][:].indirect(n4_t[:]), ACT.Copy)

        def fetch_gate(t):
            nc.vector.tensor_tensor(d_win[t][:, :S], d_win[t][:, S:], h_ps[t][:], ALU.subtract)
            for places in halves if t == PACK - 1 else [slice(0, S)]:
                entries = n5_t[:, places.start // 16 : places.stop // 16]
                nc.scalar.activation(gate[:, t, places], d_win[t][:].indirect(entries), ACT.Sigmoid)

        def store(t):
            for places in halves if t == PACK - 1 else [slice(0, S)]:
                nc.vector.tensor_tensor(res[t][:, places], gate[:, t, places], h_ps[t][:, places], ALU.mult)
                nc.sync.dma_start(out_rows[:, t, places], res[t][:, places])

        close_h(0)
        for step in range(PACK + 2):
            if step + 1 < PACK:
                close_h(step + 1)
            if step < PACK:
                fetch_h(step)
            if 0 <= step - 1 < PACK:
                fetch_gate(step - 1)
            if 0 <= step - 2 < PACK:
                store(step - 2)
